import numpy as np
import ml_dtypes


def mxq(x, axis, fmt="e4m3"):
    dtype, down = {"e4m3": (ml_dtypes.float8_e4m3fn, 7), "e5m2": (ml_dtypes.float8_e5m2, 14)}[fmt]
    v = np.moveaxis(np.asarray(x, np.float32).astype(ml_dtypes.bfloat16).astype(np.float64), axis, -1)
    blocks = v.reshape(v.shape[:-1] + (-1, 32))
    amax = np.abs(blocks).max(-1, keepdims=True)
    byte = np.maximum(np.where(amax > 0, np.frexp(amax)[1] - 1 + 127, 0) - down, 1)
    scale = np.exp2(byte - 127.0)
    codes = (blocks / scale).astype(np.float32).astype(dtype).astype(np.float64)
    return np.moveaxis((codes * scale).reshape(v.shape), -1, axis)


WIDE = False


def mx_kscale(k):
    if not WIDE:
        return np.ones(k)
    levels = np.array([10, -10, 5, -5, 0])
    if k % 512:
        return np.exp2(np.random.permutation(np.resize(levels, k // 32))).repeat(32)
    a = np.empty((k // 512, 16))
    for p in range(k // 512):
        a[p, :8] = np.random.permutation(np.resize(levels, 8))
        for g in range(8):
            far = levels[np.abs(levels - a[p, g]) >= 10]
            a[p, g + 8] = far[np.random.randint(len(far))]
    return np.exp2(a.ravel()).repeat(32)


def f64(x):
    return np.asarray(x).astype(np.float64)


def striped(idx):
    return np.tile(idx.reshape(-1, 16).T, (8, 1)).astype(np.uint16)


def unstriped(offs):
    return offs[:16].T.reshape(-1).astype(np.int64)


def striped8(idx):
    return np.concatenate([x.reshape(-1, 16).T for x in idx]).astype(np.uint16)


def runs(offs, k):
    lists = np.stack([offs[16 * r : 16 * r + 16].T.reshape(-1) for r in range(8)]).astype(np.int64)
    return lists[np.arange(k) % 512 // 64]


def pack_weight(w):
    k, n = w.shape
    w = f64(np.asarray(w, np.float32).astype(ml_dtypes.bfloat16)).reshape(k // 32, 32, n)
    amax = np.abs(w).max(1)
    byte = np.clip(np.where(amax > 0, np.frexp(amax)[1] - 1 + 127 - 7, 1), 1, 254)
    scaled = (w * np.exp2(127.0 - byte)[:, None, :]).reshape(k, n).astype(np.float32)
    words = np.ascontiguousarray(scaled.reshape(k // 512, 128, 4, n).transpose(0, 1, 3, 2)).astype(ml_dtypes.float8_e4m3fn).view(np.uint8)
    return words, np.ascontiguousarray(byte.astype(np.uint8).reshape(k // 512, 16, n))


def unpack_weight(words, scales):
    g, p, n, _ = words.shape
    vals = np.ascontiguousarray(words).view(ml_dtypes.float8_e4m3fn).astype(np.float64) * np.repeat(np.exp2(scales.astype(np.float64) - 127.0), 8, axis=1)[..., None]
    return vals.transpose(0, 1, 3, 2).reshape(g * 512, n)


K, T, S, V, N, H = 512, 2048, 512, 256, 512, 512


def setup_inputs():
    n = np.random.standard_normal
    s = mx_kscale(K)[:, None]
    u = mx_kscale(H)
    packed_xT = pack_weight(n((K, T)) * s)
    perm = np.stack([np.random.permutation(S) for _ in range(8)])
    perm2 = np.stack([np.random.permutation(S) for _ in range(8)])
    return {
        "x_words": packed_xT[0],
        "x_scales": packed_xT[1],
        "w1": (n((K, H)) / np.sqrt(K) / s * u).astype(np.float32),
        "w2": (n((H, H)) / np.sqrt(H) / u[:, None] * u).astype(np.float32),
        "w3": (n((H, N)) / np.sqrt(H) / u[:, None]).astype(np.float32),
        "res": n((N, S)).astype(np.float32),
        "offs": striped(np.random.permutation(T)[:S]),
        "la": striped8(perm[:, :V]),
        "lb": striped8(perm[:, V:]),
        "ma": striped8(perm2[:, :V]),
        "mb": striped8(perm2[:, V:]),
    }


def reference(x_words, x_scales, w1, w2, w3, res, offs, la, lb, ma, mb):
    xq = unpack_weight(x_words, x_scales)[:, unstriped(offs)]
    y = mxq(f64(w1), 0, "e4m3").T @ xq
    nb = 0.5 * (y[np.arange(H)[:, None], runs(la, H)] + y[np.arange(H)[:, None], runs(lb, H)])
    na = y[np.arange(H)[:, None], runs(lb, H)] - (y[np.arange(H)[:, None], runs(la, H)])
    p0 = np.zeros((H, S))
    p0[np.arange(H)[:, None], runs(la, H)] = na
    z = p0.copy()
    z[np.arange(H)[:, None], runs(lb, H)] = nb
    h = mxq(f64(w2), 0, "e4m3").T @ mxq(z, 0, "e4m3")
    rb = np.minimum(h[np.arange(H)[:, None], runs(ma, H)], h[np.arange(H)[:, None], runs(mb, H)])
    ra = np.maximum(h[np.arange(H)[:, None], runs(ma, H)], h[np.arange(H)[:, None], runs(mb, H)])
    q0 = np.zeros((H, S))
    q0[np.arange(H)[:, None], runs(ma, H)] = ra
    z2 = q0.copy()
    z2[np.arange(H)[:, None], runs(mb, H)] = rb
    return f64(res) + (mxq(f64(w3), 0, "e4m3").T @ mxq(z2, 0, "e4m3"))

@@ -1,0 +1,209 @@
+from contextlib import ExitStack
+
+import concourse.mybir as mybir
+
+K, T, S, V, N, H = 512, 2048, 512, 256, 512, 512
+FLOPS = 2 * S * (K * H + H * H + H * N)
+
+F32 = mybir.dt.float32
+BF16 = mybir.dt.bfloat16
+I32 = mybir.dt.int32
+U32 = mybir.dt.uint32
+U16 = mybir.dt.uint16
+U8 = mybir.dt.uint8
+FP8X4 = mybir.dt.float8_e4m3fn_x4
+ALU = mybir.AluOpType
+ACT = mybir.ActivationFunctionType
+
+P = 128
+PACK = 4
+CHUNK = 128
+CHUNKS = S // CHUNK
+HALF = S // 2
+
+
+def tile_picked_lifted_none_p_kernel(
+    tc, x_words, x_scales, w1, w2, w3, res, offs, la, lb, ma, mb, out
+):
+    nc = tc.nc
+    with ExitStack() as ctx:
+        lists = ctx.enter_context(tc.tile_pool(name="lists", bufs=1))
+        sb = ctx.enter_context(tc.tile_pool(name="sb", bufs=1))
+        psum = ctx.enter_context(tc.psum_pool(name="psum", bufs=1))
+
+        def alloc(shape, dtype, name, tag=None):
+            return sb.tile(shape, dtype, name=name, tag=tag or name, align_bytes=64)
+
+        def bank(b, name):
+            return psum.tile([P, 512], F32, name=name, tag="bank%d" % b)
+
+        def load_list(src, name):
+            t = lists.tile(list(src.shape), U16, name=name)
+            nc.sync.dma_start(t[:], src)
+            return t
+
+        def product(dst, w_codes, w_scales, codes, scales):
+            nc.tensor.matmul_mx(
+                out=dst, lhsT=w_codes.bitcast(FP8X4), lhsT_scale=w_scales,
+                rhs=codes.bitcast(FP8X4), rhs_scale=scales, start=True, stop=True,
+            )
+
+        xs = alloc([P, T], U8, "xs")
+        nc.vector.memset(xs[:].bitcast(I32), 0)
+        offs_t = load_list(offs, "offs_t")
+        w1_rows = w1.rearrange("(p j) c -> p j c", j=PACK)
+        w1_raw = [alloc([P, PACK, HALF], F32, "w1_raw%d" % u) for u in range(2)]
+        nc.sync.dma_start(w1_raw[0][:], w1_rows[:, :, 0:HALF])
+        for q in range(4):
+            nc.sync.dma_start(xs[32 * q : 32 * q + 4, :].bitcast(I32), x_scales[0, 4 * q : 4 * q + 4, :].bitcast(I32))
+        nc.sync.dma_start(w1_raw[1][:], w1_rows[:, :, HALF:H])
+        xw = alloc([P, T], I32, "xw")
+        nc.sync.dma_start(xw[:], x_words[0].rearrange("p n t -> p (n t)").bitcast(I32))
+        la_t = load_list(la, "la_t")
+        lb_t = load_list(lb, "lb_t")
+        w2_raw = alloc([P, PACK, H], F32, "w2_raw")
+        nc.sync.dma_start(w2_raw[:], w2.rearrange("(p j) c -> p j c", j=PACK))
+        ma_t = load_list(ma, "ma_t")
+        mb_t = load_list(mb, "mb_t")
+        w3_raw = alloc([P, PACK, N], F32, "w3_raw")
+        nc.sync.dma_start(w3_raw[:], w3.rearrange("(p j) c -> p j c", j=PACK))
+        res_t = alloc([P, 4, S], F32, "res_t")
+        nc.sync.dma_start(res_t[:], res.rearrange("(t p) c -> p t c", p=P))
+
+        w1_b = alloc([P, PACK * H], BF16, "w1_b")
+        w1_deal = w1_b[:].rearrange("p (a b m j) -> p m j b a", a=2, b=2, j=PACK)
+        nc.scalar.copy(w1_deal[:, 0:64], w1_raw[0][:].rearrange("p j (m b a) -> p m j b a", a=2, b=2))
+        xs_g = alloc([P, S], U8, "xs_g")
+        nc.vector.tensor_copy(xs_g[:], xs[:].indirect(offs_t[:]))
+        nc.vector.tensor_copy(w1_deal[:, 64:128], w1_raw[1][:].rearrange("p j (m b a) -> p m j b a", a=2, b=2))
+        w1_c = alloc([P, H], U32, "w1_c")
+        w1_s = alloc([P, H], U8, "w1_s")
+        nc.vector.quantize_mx(out=w1_c[:].bitcast(FP8X4), scales=w1_s[:], in_=w1_b[:])
+        xw_g = alloc([P, S], U32, "xw_g")
+        y = [alloc([P, S], F32, "y%d" % t) for t in range(4)]
+        for u in range(2):
+            cols = slice(u * HALF, (u + 1) * HALF)
+            nc.vector.tensor_copy(xw_g[:, cols], xw[:].bitcast(U32).indirect(offs_t[:, 16 * u : 16 * (u + 1)]))
+            acc = bank(u, "y_acc0%d" % u)
+            product(acc[:, 0:HALF], w1_c[:, 0:P], w1_s[:, 0:P], xw_g[:, cols], xs_g[:, cols])
+            nc.scalar.copy(y[0][:, cols], acc[:, 0:HALF])
+        for t in range(1, 4):
+            acc = bank(1 + t, "y_acc%d" % t)
+            product(acc[:], w1_c[:, t * P : (t + 1) * P], w1_s[:, t * P : (t + 1) * P], xw_g[:], xs_g[:])
+            nc.scalar.copy(y[t][:], acc[:])
+
+        w2_b = alloc([P, PACK * H], BF16, "w2_b")
+        w3_b = alloc([P, PACK * N], BF16, "w3_b")
+
+        def cast_w2(i):
+            dst = w2_b[:].rearrange("p (a b m j) -> p m j b a", a=2, b=2, j=PACK)
+            srcv = w2_raw[:].rearrange("p j (m b a) -> p m j b a", a=2, b=2)
+            nc.scalar.copy(dst[:, 32 * i : 32 * (i + 1)], srcv[:, 32 * i : 32 * (i + 1)])
+
+        def cast_w3(i):
+            dst = w3_b[:].rearrange("p (c i j) -> p c j i", i=4, j=PACK)
+            srcv = w3_raw[:].rearrange("p j (c i) -> p c j i", i=4)
+            nc.scalar.copy(dst[:, 32 * i : 32 * (i + 1)], srcv[:, 32 * i : 32 * (i + 1)])
+
+        def pair_step(stage, rows, first, second, spare, filler):
+            z = [alloc([P, S], F32, "z%d%d" % (stage, t)) for t in range(4)]
+            zb = [alloc([P, HALF, PACK], BF16, "zb%d%d" % (stage, u)) for u in range(2)]
+            for pair in range(2):
+                ts = (2 * pair, 2 * pair + 1)
+                a, d, up, down = {}, {}, {}, {}
+                for t in ts:
+                    a[t] = alloc([P, V], F32, "a%d%d" % (stage, t), "a%d%d" % (stage, t % 2))
+                    nc.vector.tensor_copy(a[t][:], rows[t][:].indirect(first[:]))
+                for t in ts:
+                    d[t] = alloc([P, V], F32, "d%d%d" % (stage, t), "d%d%d" % (stage, t % 2))
+                    nc.vector.tensor_tensor(d[t][:], rows[t][:].indirect(second[:]), a[t][:], ALU.subtract)
+                    down[t] = alloc([P, V], F32, "down%d%d" % (stage, t), "down%d%d" % (stage, t % 2))
+                    if stage == 0:
+                        nc.scalar.activation(down[t][:], d[t][:], ACT.Copy, scale=0.5)
+                    else:
+                        up[t] = alloc([P, V], F32, "up%d" % t, "up%d" % (t % 2))
+                        nc.scalar.activation(up[t][:], d[t][:], ACT.Relu)
+                if stage == 1:
+                    for t in ts:
+                        neg = alloc([P, V], F32, "neg%d" % t, "neg")
+                        nc.scalar.activation(neg[:], d[t][:], ACT.Relu, scale=-1.0)
+                        nc.scalar.activation(down[t][:], neg[:], ACT.Copy, scale=-1.0)
+                for t in ts:
+                    if stage == 0:
+                        nc.vector.tensor_copy(z[t][:].indirect(first[:]), d[t][:])
+                    else:
+                        nc.vector.tensor_tensor(z[t][:].indirect(first[:]), a[t][:], up[t][:], ALU.add)
+                for t in ts:
+                    nc.vector.tensor_tensor(z[t][:].indirect(second[:]), a[t][:], down[t][:], ALU.add)
+                    slot = 2 * (t % 2) + t // 2
+                    if t < 3:
+                        for u in range(2):
+                            nc.scalar.copy(zb[u][:, :, slot], z[t][:, u * HALF : (u + 1) * HALF])
+                    else:
+                        filler()
+                        for c in range(CHUNKS):
+                            dst = zb[c // 2][:, (c % 2) * CHUNK : (c % 2 + 1) * CHUNK, slot]
+                            if c < 2:
+                                nc.vector.tensor_copy(dst, z[t][:, c * CHUNK : (c + 1) * CHUNK])
+                            else:
+                                nc.scalar.copy(dst, z[t][:, c * CHUNK : (c + 1) * CHUNK])
+                if pair == 0:
+                    spare()
+            return zb
+
+        def quantise_w(src, t0, count, name, tag):
+            codes = alloc([P, count * P], U32, name + "_c", tag)
+            scales = alloc([P, count * P], U8, name + "_s")
+            nc.vector.quantize_mx(out=codes[:].bitcast(FP8X4), scales=scales[:], in_=src[:, t0 * PACK * P : (t0 + count) * PACK * P])
+            return [(codes[:, i * P : (i + 1) * P], scales[:, i * P : (i + 1) * P]) for i in range(count)]
+
+        def quantise_z(zb, codes, scales, c0, count):
+            cols = slice(c0 * CHUNK, (c0 + count) * CHUNK)
+            src = zb[c0 // 2][:].rearrange("p n j -> p (n j)")
+            nc.vector.quantize_mx(
+                out=codes[:, cols].bitcast(FP8X4), scales=scales[:, cols],
+                in_=src[:, (c0 % 2) * PACK * CHUNK : (c0 % 2 + count) * PACK * CHUNK],
+            )
+
+        def casts():
+            for i in range(4):
+                cast_w2(i)
+            for i in range(4):
+                cast_w3(i)
+
+        w2_q, w3_q = [], []
+        zb = pair_step(0, y, la_t, lb_t, casts, lambda: w2_q.extend(quantise_w(w2_b, 0, 1, "w2_0", "a00")))
+
+        z_c = alloc([P, S], U32, "z_c")
+        z_s = alloc([P, S], U8, "z_s")
+        h = [alloc([P, S], F32, "h%d" % t) for t in range(4)]
+        for u in range(2):
+            acc = bank(u, "h_acc0%d" % u)
+            for c in range(2 * u, 2 * u + 2):
+                cols = slice(c * CHUNK, (c + 1) * CHUNK)
+                quantise_z(zb, z_c, z_s, c, 1)
+                product(acc[:, (c % 2) * CHUNK : (c % 2 + 1) * CHUNK], w2_q[0][0], w2_q[0][1], z_c[:, cols], z_s[:, cols])
+            nc.scalar.copy(h[0][:, u * HALF : (u + 1) * HALF], acc[:, 0:HALF])
+        w2_q.extend(quantise_w(w2_b, 1, 1, "w2_1", "a01"))
+        w2_q.extend(quantise_w(w2_b, 2, 2, "w2_hi", "down01"))
+        for t in range(1, 4):
+            acc = bank(1 + t, "h_acc%d" % t)
+            product(acc[:], w2_q[t][0], w2_q[t][1], z_c[:], z_s[:])
+            nc.scalar.copy(h[t][:], acc[:])
+        w3_q.extend(quantise_w(w3_b, 0, 2, "w3_lo", "z03"))
+
+        zb2 = pair_step(1, h, ma_t, mb_t, lambda: None, lambda: w3_q.extend(quantise_w(w3_b, 2, 2, "w3_hi", "a10")))
+
+        z2_c = alloc([P, S], U32, "z2_c")
+        z2_s = alloc([P, S], U8, "z2_s")
+        for c in range(2):
+            quantise_z(zb2, z2_c, z2_s, c, 1)
+        quantise_z(zb2, z2_c, z2_s, 2, 2)
+        for u in range(2):
+            cols = slice(u * HALF, (u + 1) * HALF)
+            for t in range(4):
+                acc = bank(4 * u + t, "o_acc%d%d" % (u, t))
+                product(acc[:, 0:HALF], w3_q[t][0], w3_q[t][1], z2_c[:, cols], z2_s[:, cols])
+                o = alloc([P, HALF], F32, "o%d%d" % (u, t))
+                nc.vector.tensor_tensor(o[:], acc[:, 0:HALF], res_t[:, t, cols], ALU.add)
+                nc.sync.dma_start(out[t * P : (t + 1) * P, cols], o[:])

@@ -48,15 +48,19 @@ def tile_picked_lifted_none_p_kernel(
                 rhs=codes.bitcast(FP8X4), rhs_scale=scales, start=True, stop=True,
             )
 
+        def quantise_w(src, t0, count, name, tag):
+            codes = alloc([P, count * P], U32, name + "_c", tag)
+            scales = alloc([P, count * P], U8, name + "_s")
+            nc.vector.quantize_mx(out=codes[:].bitcast(FP8X4), scales=scales[:], in_=src[:, t0 * PACK * P : (t0 + count) * PACK * P])
+            return [(codes[:, i * P : (i + 1) * P], scales[:, i * P : (i + 1) * P]) for i in range(count)]
+
         xs = alloc([P, T], U8, "xs")
         nc.vector.memset(xs[:].bitcast(I32), 0)
         offs_t = load_list(offs, "offs_t")
-        w1_rows = w1.rearrange("(p j) c -> p j c", j=PACK)
-        w1_raw = [alloc([P, PACK, HALF], F32, "w1_raw%d" % u) for u in range(2)]
-        nc.sync.dma_start(w1_raw[0][:], w1_rows[:, :, 0:HALF])
+        w1_raw = alloc([P, PACK, H], F32, "w1_raw")
+        nc.sync.dma_start(w1_raw[:], w1.rearrange("(p j) c -> p j c", j=PACK))
         for q in range(4):
             nc.sync.dma_start(xs[32 * q : 32 * q + 4, :].bitcast(I32), x_scales[0, 4 * q : 4 * q + 4, :].bitcast(I32))
-        nc.sync.dma_start(w1_raw[1][:], w1_rows[:, :, HALF:H])
         xw = alloc([P, T], I32, "xw")
         nc.sync.dma_start(xw[:], x_words[0].rearrange("p n t -> p (n t)").bitcast(I32))
         la_t = load_list(la, "la_t")
@@ -71,33 +75,37 @@ def tile_picked_lifted_none_p_kernel(
         nc.sync.dma_start(res_t[:], res.rearrange("(t p) c -> p t c", p=P))
 
         w1_b = alloc([P, PACK * H], BF16, "w1_b")
-        w1_deal = w1_b[:].rearrange("p (a b m j) -> p m j b a", a=2, b=2, j=PACK)
-        nc.scalar.copy(w1_deal[:, 0:64], w1_raw[0][:].rearrange("p j (m b a) -> p m j b a", a=2, b=2))
+        w1_deal = w1_b[:].rearrange("p (a b m j) -> p m b a j", a=2, b=2, j=PACK)
+        w1_src = w1_raw[:].rearrange("p j (m b a) -> p m b a j", a=2, b=2)
+        nc.scalar.copy(w1_deal[:, 0:80], w1_src[:, 0:80])
+        nc.vector.tensor_copy(
+            w1_b[:].rearrange("p (a b m j) -> p m j b a", a=2, b=2, j=PACK)[:, 80:128],
+            w1_raw[:].rearrange("p j (m b a) -> p m j b a", a=2, b=2)[:, 80:128],
+        )
         xs_g = alloc([P, S], U8, "xs_g")
         nc.vector.tensor_copy(xs_g[:], xs[:].indirect(offs_t[:]))
-        nc.vector.tensor_copy(w1_deal[:, 64:128], w1_raw[1][:].rearrange("p j (m b a) -> p m j b a", a=2, b=2))
-        w1_c = alloc([P, H], U32, "w1_c")
-        w1_s = alloc([P, H], U8, "w1_s")
-        nc.vector.quantize_mx(out=w1_c[:].bitcast(FP8X4), scales=w1_s[:], in_=w1_b[:])
+        w1_q = quantise_w(w1_b, 0, 2, "w1_lo", None) + quantise_w(w1_b, 2, 2, "w1_hi", None)
         xw_g = alloc([P, S], U32, "xw_g")
         y = [alloc([P, S], F32, "y%d" % t) for t in range(4)]
         for u in range(2):
             cols = slice(u * HALF, (u + 1) * HALF)
             nc.vector.tensor_copy(xw_g[:, cols], xw[:].bitcast(U32).indirect(offs_t[:, 16 * u : 16 * (u + 1)]))
-            acc = bank(u, "y_acc0%d" % u)
-            product(acc[:, 0:HALF], w1_c[:, 0:P], w1_s[:, 0:P], xw_g[:, cols], xs_g[:, cols])
-            nc.scalar.copy(y[0][:, cols], acc[:, 0:HALF])
+            for b, c0, count in (((0, 0, 2),), ((1, 2, 1), (5, 3, 1)))[u]:
+                cols = slice(c0 * CHUNK, (c0 + count) * CHUNK)
+                acc = bank(b, "y_acc0%d" % c0)
+                product(acc[:, 0 : count * CHUNK], w1_q[0][0], w1_q[0][1], xw_g[:, cols], xs_g[:, cols])
+                nc.scalar.copy(y[0][:, cols], acc[:, 0 : count * CHUNK])
         for t in range(1, 4):
             acc = bank(1 + t, "y_acc%d" % t)
-            product(acc[:], w1_c[:, t * P : (t + 1) * P], w1_s[:, t * P : (t + 1) * P], xw_g[:], xs_g[:])
+            product(acc[:], w1_q[t][0], w1_q[t][1], xw_g[:], xs_g[:])
             nc.scalar.copy(y[t][:], acc[:])
 
-        w2_b = alloc([P, PACK * H], BF16, "w2_b")
+        w2_b = alloc([P, PACK * H], BF16, "w2_b", "w1_lo_c")
         w3_b = alloc([P, PACK * N], BF16, "w3_b")
 
         def cast_w2(i):
-            dst = w2_b[:].rearrange("p (a b m j) -> p m j b a", a=2, b=2, j=PACK)
-            srcv = w2_raw[:].rearrange("p j (m b a) -> p m j b a", a=2, b=2)
+            dst = w2_b[:].rearrange("p (a b m j) -> p m b a j", a=2, b=2, j=PACK)
+            srcv = w2_raw[:].rearrange("p j (m b a) -> p m b a j", a=2, b=2)
             nc.scalar.copy(dst[:, 32 * i : 32 * (i + 1)], srcv[:, 32 * i : 32 * (i + 1)])
 
         def cast_w3(i):
@@ -105,33 +113,41 @@ def tile_picked_lifted_none_p_kernel(
             srcv = w3_raw[:].rearrange("p j (c i) -> p c j i", i=4)
             nc.scalar.copy(dst[:, 32 * i : 32 * (i + 1)], srcv[:, 32 * i : 32 * (i + 1)])
 
-        def pair_step(stage, rows, first, second, spare, filler):
+        def pair_step(stage, rows, first, second, held, spare, filler):
             z = [alloc([P, S], F32, "z%d%d" % (stage, t)) for t in range(4)]
             zb = [alloc([P, HALF, PACK], BF16, "zb%d%d" % (stage, u)) for u in range(2)]
             for pair in range(2):
                 ts = (2 * pair, 2 * pair + 1)
-                a, d, up, down = {}, {}, {}, {}
+                a, d, up, neg, down = {}, {}, {}, {}, {}
                 for t in ts:
-                    a[t] = alloc([P, V], F32, "a%d%d" % (stage, t), "a%d%d" % (stage, t % 2))
+                    if pair == 0:
+                        tag = "a%d%d" % (stage, t)
+                    else:
+                        tag = held[t % 2] if stage == 0 else "neg%d" % (t % 2)
+                    a[t] = alloc([P, V], F32, "a%d%d" % (stage, t), tag)
                     nc.vector.tensor_copy(a[t][:], rows[t][:].indirect(first[:]))
                 for t in ts:
-                    d[t] = alloc([P, V], F32, "d%d%d" % (stage, t), "d%d%d" % (stage, t % 2))
+                    tag = held[t] if pair == 0 else "a%d%d" % (stage, t % 2)
+                    d[t] = alloc([P, V], F32, "d%d%d" % (stage, t), tag)
                     nc.vector.tensor_tensor(d[t][:], rows[t][:].indirect(second[:]), a[t][:], ALU.subtract)
-                    down[t] = alloc([P, V], F32, "down%d%d" % (stage, t), "down%d%d" % (stage, t % 2))
                     if stage == 0:
+                        down[t] = alloc([P, V], F32, "down0%d" % t, "down0%d" % (t % 2))
                         nc.scalar.activation(down[t][:], d[t][:], ACT.Copy, scale=0.5)
                     else:
                         up[t] = alloc([P, V], F32, "up%d" % t, "up%d" % (t % 2))
                         nc.scalar.activation(up[t][:], d[t][:], ACT.Relu)
-                if stage == 1:
+                if stage == 0:
+                    spare(pair)
                     for t in ts:
-                        neg = alloc([P, V], F32, "neg%d" % t, "neg")
-                        nc.scalar.activation(neg[:], d[t][:], ACT.Relu, scale=-1.0)
-                        nc.scalar.activation(down[t][:], neg[:], ACT.Copy, scale=-1.0)
-                for t in ts:
-                    if stage == 0:
                         nc.vector.tensor_copy(z[t][:].indirect(first[:]), d[t][:])
-                    else:
+                else:
+                    for t in ts:
+                        neg[t] = alloc([P, V], F32, "neg%d" % t)
+                        nc.scalar.activation(neg[t][:], d[t][:], ACT.Relu, scale=-1.0)
+                    for t in ts:
+                        down[t] = alloc([P, V], F32, "down1%d" % t, "down1%d" % (t % 2))
+                        nc.scalar.activation(down[t][:], neg[t][:], ACT.Copy, scale=-1.0)
+                    for t in ts:
                         nc.vector.tensor_tensor(z[t][:].indirect(first[:]), a[t][:], up[t][:], ALU.add)
                 for t in ts:
                     nc.vector.tensor_tensor(z[t][:].indirect(second[:]), a[t][:], down[t][:], ALU.add)
@@ -147,15 +163,7 @@ def tile_picked_lifted_none_p_kernel(
                                 nc.vector.tensor_copy(dst, z[t][:, c * CHUNK : (c + 1) * CHUNK])
                             else:
                                 nc.scalar.copy(dst, z[t][:, c * CHUNK : (c + 1) * CHUNK])
-                if pair == 0:
-                    spare()
             return zb
-
-        def quantise_w(src, t0, count, name, tag):
-            codes = alloc([P, count * P], U32, name + "_c", tag)
-            scales = alloc([P, count * P], U8, name + "_s")
-            nc.vector.quantize_mx(out=codes[:].bitcast(FP8X4), scales=scales[:], in_=src[:, t0 * PACK * P : (t0 + count) * PACK * P])
-            return [(codes[:, i * P : (i + 1) * P], scales[:, i * P : (i + 1) * P]) for i in range(count)]
 
         def quantise_z(zb, codes, scales, c0, count):
             cols = slice(c0 * CHUNK, (c0 + count) * CHUNK)
@@ -165,26 +173,27 @@ def tile_picked_lifted_none_p_kernel(
                 in_=src[:, (c0 % 2) * PACK * CHUNK : (c0 % 2 + count) * PACK * CHUNK],
             )
 
-        def casts():
-            for i in range(4):
-                cast_w2(i)
-            for i in range(4):
-                cast_w3(i)
+        def casts(pair):
+            if pair == 0:
+                for i in range(4):
+                    cast_w2(i)
+                for i in range(4):
+                    cast_w3(i)
 
         w2_q, w3_q = [], []
-        zb = pair_step(0, y, la_t, lb_t, casts, lambda: w2_q.extend(quantise_w(w2_b, 0, 1, "w2_0", "a00")))
+        zb = pair_step(0, y, la_t, lb_t, ("w1_hi_c", "w1_hi_s"), casts, lambda: w2_q.extend(quantise_w(w2_b, 0, 1, "w2_0", "w1_hi_c")))
 
         z_c = alloc([P, S], U32, "z_c")
         z_s = alloc([P, S], U8, "z_s")
         h = [alloc([P, S], F32, "h%d" % t) for t in range(4)]
-        for u in range(2):
-            acc = bank(u, "h_acc0%d" % u)
-            for c in range(2 * u, 2 * u + 2):
+        for b, c0, count in ((0, 0, 2), (1, 2, 1), (5, 3, 1)):
+            acc = bank(b, "h_acc0%d" % c0)
+            for c in range(c0, c0 + count):
                 cols = slice(c * CHUNK, (c + 1) * CHUNK)
                 quantise_z(zb, z_c, z_s, c, 1)
-                product(acc[:, (c % 2) * CHUNK : (c % 2 + 1) * CHUNK], w2_q[0][0], w2_q[0][1], z_c[:, cols], z_s[:, cols])
-            nc.scalar.copy(h[0][:, u * HALF : (u + 1) * HALF], acc[:, 0:HALF])
-        w2_q.extend(quantise_w(w2_b, 1, 1, "w2_1", "a01"))
+                product(acc[:, (c - c0) * CHUNK : (c - c0 + 1) * CHUNK], w2_q[0][0], w2_q[0][1], z_c[:, cols], z_s[:, cols])
+            nc.scalar.copy(h[0][:, c0 * CHUNK : (c0 + count) * CHUNK], acc[:, 0 : count * CHUNK])
+        w2_q.extend(quantise_w(w2_b, 1, 1, "w2_1", "w1_hi_s"))
         w2_q.extend(quantise_w(w2_b, 2, 2, "w2_hi", "down01"))
         for t in range(1, 4):
             acc = bank(1 + t, "h_acc%d" % t)
@@ -192,13 +201,14 @@ def tile_picked_lifted_none_p_kernel(
             nc.scalar.copy(h[t][:], acc[:])
         w3_q.extend(quantise_w(w3_b, 0, 2, "w3_lo", "z03"))
 
-        zb2 = pair_step(1, h, ma_t, mb_t, lambda: None, lambda: w3_q.extend(quantise_w(w3_b, 2, 2, "w3_hi", "a10")))
+        zb2 = pair_step(1, h, ma_t, mb_t, ("down01", "z_c"), None, lambda: w3_q.extend(quantise_w(w3_b, 2, 1, "w3_2", "neg0")))
 
         z2_c = alloc([P, S], U32, "z2_c")
         z2_s = alloc([P, S], U8, "z2_s")
         for c in range(2):
             quantise_z(zb2, z2_c, z2_s, c, 1)
         quantise_z(zb2, z2_c, z2_s, 2, 2)
+        w3_q.extend(quantise_w(w3_b, 3, 1, "w3_3", "neg1"))
         for u in range(2):
             cols = slice(u * HALF, (u + 1) * HALF)
             for t in range(4):

@@ -56,11 +56,11 @@ def tile_picked_lifted_none_p_kernel(
 
         xs = alloc([P, T], U8, "xs")
         nc.vector.memset(xs[:].bitcast(I32), 0)
-        offs_t = load_list(offs, "offs_t")
         w1_raw = alloc([P, PACK, H], F32, "w1_raw")
         nc.sync.dma_start(w1_raw[:], w1.rearrange("(p j) c -> p j c", j=PACK))
-        for q in range(4):
-            nc.sync.dma_start(xs[32 * q : 32 * q + 4, :].bitcast(I32), x_scales[0, 4 * q : 4 * q + 4, :].bitcast(I32))
+        offs_t = load_list(offs, "offs_t")
+        for r in range(4):
+            nc.sync.dma_start(xs[r:P:32, :].bitcast(I32), x_scales[0, r:16:4, :].bitcast(I32))
         xw = alloc([P, T], I32, "xw")
         nc.sync.dma_start(xw[:], x_words[0].rearrange("p n t -> p (n t)").bitcast(I32))
         la_t = load_list(la, "la_t")
@@ -78,10 +78,7 @@ def tile_picked_lifted_none_p_kernel(
         w1_deal = w1_b[:].rearrange("p (a b m j) -> p m b a j", a=2, b=2, j=PACK)
         w1_src = w1_raw[:].rearrange("p j (m b a) -> p m b a j", a=2, b=2)
         nc.scalar.copy(w1_deal[:, 0:80], w1_src[:, 0:80])
-        nc.vector.tensor_copy(
-            w1_b[:].rearrange("p (a b m j) -> p m j b a", a=2, b=2, j=PACK)[:, 80:128],
-            w1_raw[:].rearrange("p j (m b a) -> p m j b a", a=2, b=2)[:, 80:128],
-        )
+        nc.vector.tensor_copy(w1_deal[:, 80:128], w1_src[:, 80:128])
         xs_g = alloc([P, S], U8, "xs_g")
         nc.vector.tensor_copy(xs_g[:], xs[:].indirect(offs_t[:]))
         w1_q = quantise_w(w1_b, 0, 2, "w1_lo", None) + quantise_w(w1_b, 2, 2, "w1_hi", None)

@@ -17,9 +17,12 @@ ACT = mybir.ActivationFunctionType
 
 P = 128
 PACK = 4
-CHUNK = 128
-CHUNKS = S // CHUNK
 HALF = S // 2
+QUARTER = S // 4
+LIST_ROWS = 16
+SLOT = (0, 2, 1, 3)
+W1_ON_SCALAR = 80
+CAST_PIECES = 4
 
 
 def tile_picked_lifted_none_p_kernel(
@@ -31,186 +34,225 @@ def tile_picked_lifted_none_p_kernel(
         sb = ctx.enter_context(tc.tile_pool(name="sb", bufs=1))
         psum = ctx.enter_context(tc.psum_pool(name="psum", bufs=1))
 
-        def alloc(shape, dtype, name, tag=None):
-            return sb.tile(shape, dtype, name=name, tag=tag or name, align_bytes=64)
+        def alloc(shape, dtype, name, takes_over=None):
+            return sb.tile(shape, dtype, name=name, tag=takes_over or name, align_bytes=64)
 
         def bank(b, name):
-            return psum.tile([P, 512], F32, name=name, tag="bank%d" % b)
+            return psum.tile([P, S], F32, name=name, tag="bank%d" % b)
 
         def load_list(src, name):
-            t = lists.tile(list(src.shape), U16, name=name)
-            nc.sync.dma_start(t[:], src)
-            return t
+            offsets = lists.tile(list(src.shape), U16, name=name)
+            nc.sync.dma_start(offsets[:], src)
+            return offsets
 
-        def product(dst, w_codes, w_scales, codes, scales):
+        def load_weight(w, name):
+            raw = alloc([P, PACK, w.shape[1]], F32, name)
+            nc.sync.dma_start(raw[:], w.rearrange("(p j) c -> p j c", j=PACK))
+            return raw
+
+        def dealt_views(rounded, raw):
+            return (
+                rounded[:].rearrange("p (a b m j) -> p m b a j", a=2, b=2, j=PACK),
+                raw[:].rearrange("p j (m b a) -> p m b a j", a=2, b=2),
+            )
+
+        def quantise_weight(rounded, first, count, name, takes_over=None, scales=None):
+            codes = alloc([P, count * P], U32, name + "_codes", takes_over)
+            if scales is None:
+                scales = alloc([P, count * P], U8, name + "_scales")[:]
+            nc.vector.quantize_mx(
+                out=codes[:].bitcast(FP8X4), scales=scales, in_=rounded[:, first * PACK * P : (first + count) * PACK * P]
+            )
+            return [(codes[:, g * P : (g + 1) * P], scales[:, g * P : (g + 1) * P]) for g in range(count)]
+
+        def quantise_places(halves, codes, scales, first, count):
+            cols = slice(first * QUARTER, (first + count) * QUARTER)
+            words = halves[first // 2][:].rearrange("p n j -> p (n j)")
+            nc.vector.quantize_mx(
+                out=codes[:, cols].bitcast(FP8X4),
+                scales=scales[:, cols],
+                in_=words[:, (first % 2) * PACK * QUARTER : (first % 2 + count) * PACK * QUARTER],
+            )
+
+        def product(dst, weight, codes, scales):
             nc.tensor.matmul_mx(
-                out=dst, lhsT=w_codes.bitcast(FP8X4), lhsT_scale=w_scales,
+                out=dst, lhsT=weight[0].bitcast(FP8X4), lhsT_scale=weight[1],
                 rhs=codes.bitcast(FP8X4), rhs_scale=scales, start=True, stop=True,
             )
 
-        def quantise_w(src, t0, count, name, tag):
-            codes = alloc([P, count * P], U32, name + "_c", tag)
-            scales = alloc([P, count * P], U8, name + "_s")
-            nc.vector.quantize_mx(out=codes[:].bitcast(FP8X4), scales=scales[:], in_=src[:, t0 * PACK * P : (t0 + count) * PACK * P])
-            return [(codes[:, i * P : (i + 1) * P], scales[:, i * P : (i + 1) * P]) for i in range(count)]
+        def product_to_rows(b, name, rows, cols, weight, codes, scales):
+            width = cols.stop - cols.start
+            acc = bank(b, name)
+            product(acc[:, 0:width], weight, codes[:, cols], scales[:, cols])
+            nc.scalar.copy(rows[:, cols], acc[:, 0:width])
 
-        xs = alloc([P, T], U8, "xs")
-        nc.vector.memset(xs[:].bitcast(I32), 0)
-        w1_raw = alloc([P, PACK, H], F32, "w1_raw")
-        nc.sync.dma_start(w1_raw[:], w1.rearrange("(p j) c -> p j c", j=PACK))
+        def gather(rows, offsets, name, takes_over=None):
+            picked = alloc([P, V], F32, name, takes_over)
+            nc.vector.tensor_copy(picked[:], rows[:].indirect(offsets[:]))
+            return picked
+
+        def gather_less(rows, offsets, other, name, takes_over=None):
+            diff = alloc([P, V], F32, name, takes_over)
+            nc.vector.tensor_tensor(diff[:], rows[:].indirect(offsets[:]), other[:], ALU.subtract)
+            return diff
+
+        def apply(func, scale, src, name, takes_over=None):
+            dst = alloc([P, V], F32, name, takes_over)
+            nc.scalar.activation(dst[:], src[:], func, scale=scale)
+            return dst
+
+        def scatter_sum(rows, offsets, left, right):
+            nc.vector.tensor_tensor(rows[:].indirect(offsets[:]), left[:], right[:], ALU.add)
+
+        def interleave(halves, rows, i):
+            for u in range(2):
+                nc.scalar.copy(halves[u][:, :, SLOT[i]], rows[:, u * HALF : (u + 1) * HALF])
+
+        def interleave_last(halves, rows):
+            for c in range(4):
+                dst = halves[c // 2][:, (c % 2) * QUARTER : (c % 2 + 1) * QUARTER, SLOT[3]]
+                copy = nc.vector.tensor_copy if c < 2 else nc.scalar.copy
+                copy(dst, rows[:, c * QUARTER : (c + 1) * QUARTER])
+
+        x_scale_rows = alloc([P, T], U8, "x_scale_rows")
+        nc.vector.memset(x_scale_rows[:].bitcast(I32), 0)
+        w1_raw = load_weight(w1, "w1_raw")
         offs_t = load_list(offs, "offs_t")
         for r in range(4):
-            nc.sync.dma_start(xs[r:P:32, :].bitcast(I32), x_scales[0, r:16:4, :].bitcast(I32))
-        xw = alloc([P, T], I32, "xw")
-        nc.sync.dma_start(xw[:], x_words[0].rearrange("p n t -> p (n t)").bitcast(I32))
+            nc.sync.dma_start(x_scale_rows[r:P:32, :].bitcast(I32), x_scales[0, r:16:4, :].bitcast(I32))
+        x_table = alloc([P, T], I32, "x_table")
+        nc.sync.dma_start(x_table[:], x_words[0].rearrange("p n t -> p (n t)").bitcast(I32))
         la_t = load_list(la, "la_t")
         lb_t = load_list(lb, "lb_t")
-        w2_raw = alloc([P, PACK, H], F32, "w2_raw")
-        nc.sync.dma_start(w2_raw[:], w2.rearrange("(p j) c -> p j c", j=PACK))
+        w2_raw = load_weight(w2, "w2_raw")
         ma_t = load_list(ma, "ma_t")
         mb_t = load_list(mb, "mb_t")
-        w3_raw = alloc([P, PACK, N], F32, "w3_raw")
-        nc.sync.dma_start(w3_raw[:], w3.rearrange("(p j) c -> p j c", j=PACK))
-        res_t = alloc([P, 4, S], F32, "res_t")
+        w3_raw = load_weight(w3, "w3_raw")
+        res_t = alloc([P, N // P, S], F32, "res_t")
         nc.sync.dma_start(res_t[:], res.rearrange("(t p) c -> p t c", p=P))
 
-        w1_b = alloc([P, PACK * H], BF16, "w1_b")
-        w1_deal = w1_b[:].rearrange("p (a b m j) -> p m b a j", a=2, b=2, j=PACK)
-        w1_src = w1_raw[:].rearrange("p j (m b a) -> p m b a j", a=2, b=2)
-        nc.scalar.copy(w1_deal[:, 0:80], w1_src[:, 0:80])
-        nc.vector.tensor_copy(w1_deal[:, 80:128], w1_src[:, 80:128])
-        xs_g = alloc([P, S], U8, "xs_g")
-        nc.vector.tensor_copy(xs_g[:], xs[:].indirect(offs_t[:]))
-        w1_q = quantise_w(w1_b, 0, 2, "w1_lo", None) + quantise_w(w1_b, 2, 2, "w1_hi", None)
-        xw_g = alloc([P, S], U32, "xw_g")
-        y = [alloc([P, S], F32, "y%d" % t) for t in range(4)]
+        w1_bf = alloc([P, PACK * H], BF16, "w1_bf")
+        w1_dst, w1_src = dealt_views(w1_bf, w1_raw)
+        nc.scalar.copy(w1_dst[:, 0:W1_ON_SCALAR], w1_src[:, 0:W1_ON_SCALAR])
+        nc.vector.tensor_copy(w1_dst[:, W1_ON_SCALAR:P], w1_src[:, W1_ON_SCALAR:P])
+        x_scales_picked = alloc([P, S], U8, "x_scales_picked")
+        nc.vector.tensor_copy(x_scales_picked[:], x_scale_rows[:].indirect(offs_t[:]))
+        w1_q = quantise_weight(w1_bf, 0, 2, "w1_01") + quantise_weight(w1_bf, 2, 1, "w1_2") + quantise_weight(w1_bf, 3, 1, "w1_3")
+        x_picked = alloc([P, S], U32, "x_picked")
+        y = [alloc([P, S], F32, "y%d" % i) for i in range(PACK)]
         for u in range(2):
             cols = slice(u * HALF, (u + 1) * HALF)
-            nc.vector.tensor_copy(xw_g[:, cols], xw[:].bitcast(U32).indirect(offs_t[:, 16 * u : 16 * (u + 1)]))
-            for b, c0, count in (((0, 0, 2),), ((1, 2, 1), (5, 3, 1)))[u]:
-                cols = slice(c0 * CHUNK, (c0 + count) * CHUNK)
-                acc = bank(b, "y_acc0%d" % c0)
-                product(acc[:, 0 : count * CHUNK], w1_q[0][0], w1_q[0][1], xw_g[:, cols], xs_g[:, cols])
-                nc.scalar.copy(y[0][:, cols], acc[:, 0 : count * CHUNK])
-        for t in range(1, 4):
-            acc = bank(1 + t, "y_acc%d" % t)
-            product(acc[:], w1_q[t][0], w1_q[t][1], xw_g[:], xs_g[:])
-            nc.scalar.copy(y[t][:], acc[:])
+            entries = slice(u * HALF // LIST_ROWS, (u + 1) * HALF // LIST_ROWS)
+            nc.vector.tensor_copy(x_picked[:, cols], x_table[:].bitcast(U32).indirect(offs_t[:, entries]))
+            for i in range(2):
+                product_to_rows(2 * u + i, "y_acc%d%d" % (i, u), y[i], cols, w1_q[i], x_picked, x_scales_picked)
+        for i in range(2, PACK):
+            product_to_rows(2 + i, "y_acc%d" % i, y[i], slice(0, S), w1_q[i], x_picked, x_scales_picked)
 
-        w2_b = alloc([P, PACK * H], BF16, "w2_b", "w1_lo_c")
-        w3_b = alloc([P, PACK * N], BF16, "w3_b")
+        z = [alloc([P, S], F32, "z%d" % i) for i in range(PACK)]
+        z_bf = [alloc([P, HALF, PACK], BF16, "z_bf%d" % u) for u in range(2)]
+        handed_on = ("w1_2_codes", "w1_2_scales")
+        ya, yd, yd_half = {}, {}, {}
 
-        def cast_w2(i):
-            dst = w2_b[:].rearrange("p (a b m j) -> p m b a j", a=2, b=2, j=PACK)
-            srcv = w2_raw[:].rearrange("p j (m b a) -> p m b a j", a=2, b=2)
-            nc.scalar.copy(dst[:, 32 * i : 32 * (i + 1)], srcv[:, 32 * i : 32 * (i + 1)])
+        def lift_second_gathers(tiles, buffers):
+            for i, buffer in zip(tiles, buffers):
+                yd[i] = gather_less(y[i], lb_t, ya[i], "yd%d" % i, buffer)
+                yd_half[i] = apply(ACT.Copy, 0.5, yd[i], "yd_half%d" % i, "yd_half%d" % (i % 2))
 
-        def cast_w3(i):
-            dst = w3_b[:].rearrange("p (c i j) -> p c j i", i=4, j=PACK)
-            srcv = w3_raw[:].rearrange("p j (c i) -> p c j i", i=4)
-            nc.scalar.copy(dst[:, 32 * i : 32 * (i + 1)], srcv[:, 32 * i : 32 * (i + 1)])
+        def lift_first_scatters(tiles):
+            for i in tiles:
+                nc.vector.tensor_copy(z[i][:].indirect(la_t[:]), yd[i][:])
 
-        def pair_step(stage, rows, first, second, held, spare, filler):
-            z = [alloc([P, S], F32, "z%d%d" % (stage, t)) for t in range(4)]
-            zb = [alloc([P, HALF, PACK], BF16, "zb%d%d" % (stage, u)) for u in range(2)]
-            for pair in range(2):
-                ts = (2 * pair, 2 * pair + 1)
-                a, d, up, neg, down = {}, {}, {}, {}, {}
-                for t in ts:
-                    if pair == 0:
-                        tag = "a%d%d" % (stage, t)
-                    else:
-                        tag = held[t % 2] if stage == 0 else "neg%d" % (t % 2)
-                    a[t] = alloc([P, V], F32, "a%d%d" % (stage, t), tag)
-                    nc.vector.tensor_copy(a[t][:], rows[t][:].indirect(first[:]))
-                for t in ts:
-                    tag = held[t] if pair == 0 else "a%d%d" % (stage, t % 2)
-                    d[t] = alloc([P, V], F32, "d%d%d" % (stage, t), tag)
-                    nc.vector.tensor_tensor(d[t][:], rows[t][:].indirect(second[:]), a[t][:], ALU.subtract)
-                    if stage == 0:
-                        down[t] = alloc([P, V], F32, "down0%d" % t, "down0%d" % (t % 2))
-                        nc.scalar.activation(down[t][:], d[t][:], ACT.Copy, scale=0.5)
-                    else:
-                        up[t] = alloc([P, V], F32, "up%d" % t, "up%d" % (t % 2))
-                        nc.scalar.activation(up[t][:], d[t][:], ACT.Relu)
-                if stage == 0:
-                    spare(pair)
-                    for t in ts:
-                        nc.vector.tensor_copy(z[t][:].indirect(first[:]), d[t][:])
-                else:
-                    for t in ts:
-                        neg[t] = alloc([P, V], F32, "neg%d" % t)
-                        nc.scalar.activation(neg[t][:], d[t][:], ACT.Relu, scale=-1.0)
-                    for t in ts:
-                        down[t] = alloc([P, V], F32, "down1%d" % t, "down1%d" % (t % 2))
-                        nc.scalar.activation(down[t][:], neg[t][:], ACT.Copy, scale=-1.0)
-                    for t in ts:
-                        nc.vector.tensor_tensor(z[t][:].indirect(first[:]), a[t][:], up[t][:], ALU.add)
-                for t in ts:
-                    nc.vector.tensor_tensor(z[t][:].indirect(second[:]), a[t][:], down[t][:], ALU.add)
-                    slot = 2 * (t % 2) + t // 2
-                    if t < 3:
-                        for u in range(2):
-                            nc.scalar.copy(zb[u][:, :, slot], z[t][:, u * HALF : (u + 1) * HALF])
-                    else:
-                        filler()
-                        for c in range(CHUNKS):
-                            dst = zb[c // 2][:, (c % 2) * CHUNK : (c % 2 + 1) * CHUNK, slot]
-                            if c < 2:
-                                nc.vector.tensor_copy(dst, z[t][:, c * CHUNK : (c + 1) * CHUNK])
-                            else:
-                                nc.scalar.copy(dst, z[t][:, c * CHUNK : (c + 1) * CHUNK])
-            return zb
+        for i in (0, 1):
+            ya[i] = gather(y[i], la_t, "ya%d" % i)
+        lift_second_gathers((0, 1), handed_on)
+        w2_bf = alloc([P, PACK * H], BF16, "w2_bf", "w1_01_codes")
+        w3_bf = alloc([P, PACK * N], BF16, "w3_bf")
+        w2_views = dealt_views(w2_bf, w2_raw)
+        w3_views = (
+            w3_bf[:].rearrange("p (c i j) -> p c j i", i=4, j=PACK),
+            w3_raw[:].rearrange("p j (c i) -> p c j i", i=4),
+        )
+        for dst, src in (w2_views, w3_views):
+            for piece in range(CAST_PIECES):
+                groups = slice(piece * P // CAST_PIECES, (piece + 1) * P // CAST_PIECES)
+                nc.scalar.copy(dst[:, groups], src[:, groups])
+        lift_first_scatters((0, 1))
+        for i in (0, 1):
+            scatter_sum(z[i], lb_t, ya[i], yd_half[i])
+            interleave(z_bf, z[i], i)
+        for i in (2, 3):
+            ya[i] = gather(y[i], la_t, "ya%d" % i, handed_on[i - 2])
+        lift_second_gathers((2, 3), ("ya0", "ya1"))
+        lift_first_scatters((2, 3))
+        scatter_sum(z[2], lb_t, ya[2], yd_half[2])
+        interleave(z_bf, z[2], 2)
+        scatter_sum(z[3], lb_t, ya[3], yd_half[3])
+        w2_q = quantise_weight(w2_bf, 0, 2, "w2_01", handed_on[0])
+        interleave_last(z_bf, z[3])
 
-        def quantise_z(zb, codes, scales, c0, count):
-            cols = slice(c0 * CHUNK, (c0 + count) * CHUNK)
-            src = zb[c0 // 2][:].rearrange("p n j -> p (n j)")
-            nc.vector.quantize_mx(
-                out=codes[:, cols].bitcast(FP8X4), scales=scales[:, cols],
-                in_=src[:, (c0 % 2) * PACK * CHUNK : (c0 % 2 + count) * PACK * CHUNK],
-            )
+        z_codes = alloc([P, S], U32, "z_codes")
+        z_scales = alloc([P, S], U8, "z_scales")
+        h = [alloc([P, S], F32, "h%d" % i) for i in range(PACK)]
+        for b, (first, count) in enumerate(((0, 2), (2, 1), (3, 1))):
+            acc = bank(b, "h_acc0%d" % first)
+            for c in range(first, first + count):
+                cols = slice(c * QUARTER, (c + 1) * QUARTER)
+                quantise_places(z_bf, z_codes, z_scales, c, 1)
+                product(acc[:, (c - first) * QUARTER : (c - first + 1) * QUARTER], w2_q[0], z_codes[:, cols], z_scales[:, cols])
+            nc.scalar.copy(h[0][:, first * QUARTER : (first + count) * QUARTER], acc[:, 0 : count * QUARTER])
+        late_scales = alloc([P, 4 * P], U8, "late_scales", "z_bf1")
+        for i in range(2, PACK):
+            w2_q += quantise_weight(w2_bf, i, 1, "w2_%d" % i, scales=late_scales[:, (i - 2) * P : (i - 1) * P])
+        for u in range(2):
+            product_to_rows(3 + u, "h_acc1%d" % u, h[1], slice(u * HALF, (u + 1) * HALF), w2_q[1], z_codes, z_scales)
+        for i in range(2, PACK):
+            product_to_rows(3 + i, "h_acc%d" % i, h[i], slice(0, S), w2_q[i], z_codes, z_scales)
+        w3_q = quantise_weight(w3_bf, 0, 2, "w3_01", scales=late_scales[:, 2 * P : 4 * P])
 
-        def casts(pair):
-            if pair == 0:
-                for i in range(4):
-                    cast_w2(i)
-                for i in range(4):
-                    cast_w3(i)
+        z2 = [alloc([P, S], F32, "z2%d" % i) for i in range(PACK)]
+        z2_bf = [alloc([P, HALF, PACK], BF16, "z2_bf%d" % u) for u in range(2)]
+        ha, hd, rise, fall = {}, {}, {}, {}
 
-        w2_q, w3_q = [], []
-        zb = pair_step(0, y, la_t, lb_t, ("w1_hi_c", "w1_hi_s"), casts, lambda: w2_q.extend(quantise_w(w2_b, 0, 1, "w2_0", "w1_hi_c")))
+        def sort_second_gathers(tiles, buffers):
+            for i, buffer in zip(tiles, buffers):
+                hd[i] = gather_less(h[i], mb_t, ha[i], "hd%d" % i, buffer)
+                rise[i] = apply(ACT.Relu, 1.0, hd[i], "rise%d" % i, "rise%d" % (i % 2))
 
-        z_c = alloc([P, S], U32, "z_c")
-        z_s = alloc([P, S], U8, "z_s")
-        h = [alloc([P, S], F32, "h%d" % t) for t in range(4)]
-        for b, c0, count in ((0, 0, 2), (1, 2, 1), (5, 3, 1)):
-            acc = bank(b, "h_acc0%d" % c0)
-            for c in range(c0, c0 + count):
-                cols = slice(c * CHUNK, (c + 1) * CHUNK)
-                quantise_z(zb, z_c, z_s, c, 1)
-                product(acc[:, (c - c0) * CHUNK : (c - c0 + 1) * CHUNK], w2_q[0][0], w2_q[0][1], z_c[:, cols], z_s[:, cols])
-            nc.scalar.copy(h[0][:, c0 * CHUNK : (c0 + count) * CHUNK], acc[:, 0 : count * CHUNK])
-        w2_q.extend(quantise_w(w2_b, 1, 1, "w2_1", "w1_hi_s"))
-        w2_q.extend(quantise_w(w2_b, 2, 2, "w2_hi", "down01"))
-        for t in range(1, 4):
-            acc = bank(1 + t, "h_acc%d" % t)
-            product(acc[:], w2_q[t][0], w2_q[t][1], z_c[:], z_s[:])
-            nc.scalar.copy(h[t][:], acc[:])
-        w3_q.extend(quantise_w(w3_b, 0, 2, "w3_lo", "z03"))
+        def sort_first_scatters(tiles):
+            drop = {i: apply(ACT.Relu, -1.0, hd[i], "drop%d" % i) for i in tiles}
+            for i in tiles:
+                fall[i] = apply(ACT.Copy, -1.0, drop[i], "fall%d" % i, "fall%d" % (i % 2))
+            for i in tiles:
+                scatter_sum(z2[i], ma_t, ha[i], rise[i])
 
-        zb2 = pair_step(1, h, ma_t, mb_t, ("down01", "z_c"), None, lambda: w3_q.extend(quantise_w(w3_b, 2, 1, "w3_2", "neg0")))
+        for i in (0, 1):
+            ha[i] = gather(h[i], ma_t, "ha%d" % i)
+        sort_second_gathers((0, 1), ("w2_2_codes", None))
+        sort_first_scatters((0, 1))
+        for i in (2, 3):
+            ha[i] = gather(h[i], ma_t, "ha%d" % i, "drop%d" % (i - 2))
+        scatter_sum(z2[0], mb_t, ha[0], fall[0])
+        interleave(z2_bf, z2[0], 0)
+        sort_second_gathers((2, 3), (None, None))
+        scatter_sum(z2[1], mb_t, ha[1], fall[1])
+        interleave(z2_bf, z2[1], 1)
+        sort_first_scatters((2, 3))
+        scatter_sum(z2[2], mb_t, ha[2], fall[2])
+        interleave(z2_bf, z2[2], 2)
+        scatter_sum(z2[3], mb_t, ha[3], fall[3])
+        w3_q += quantise_weight(w3_bf, 2, 2, "w3_23", "drop0")
+        interleave_last(z2_bf, z2[3])
 
-        z2_c = alloc([P, S], U32, "z2_c")
-        z2_s = alloc([P, S], U8, "z2_s")
-        for c in range(2):
-            quantise_z(zb2, z2_c, z2_s, c, 1)
-        quantise_z(zb2, z2_c, z2_s, 2, 2)
-        w3_q.extend(quantise_w(w3_b, 3, 1, "w3_3", "neg1"))
+        z2_codes = alloc([P, S], U32, "z2_codes")
+        z2_scales = alloc([P, S], U8, "z2_scales")
+        for first, count in ((0, 1), (1, 1), (2, 2)):
+            quantise_places(z2_bf, z2_codes, z2_scales, first, count)
         for u in range(2):
             cols = slice(u * HALF, (u + 1) * HALF)
-            for t in range(4):
-                acc = bank(4 * u + t, "o_acc%d%d" % (u, t))
-                product(acc[:, 0:HALF], w3_q[t][0], w3_q[t][1], z2_c[:, cols], z2_s[:, cols])
-                o = alloc([P, HALF], F32, "o%d%d" % (u, t))
-                nc.vector.tensor_tensor(o[:], acc[:, 0:HALF], res_t[:, t, cols], ALU.add)
-                nc.sync.dma_start(out[t * P : (t + 1) * P, cols], o[:])
+            for t in range(N // P):
+                acc = bank(4 * u + t, "out_acc%d%d" % (u, t))
+                product(acc[:, 0:HALF], w3_q[t], z2_codes[:, cols], z2_scales[:, cols])
+                summed = alloc([P, HALF], F32, "summed%d%d" % (u, t))
+                nc.vector.tensor_tensor(summed[:], acc[:, 0:HALF], res_t[:, t, cols], ALU.add)
+                nc.sync.dma_start(out[t * P : (t + 1) * P, cols], summed[:])

from contextlib import ExitStack

import concourse.mybir as mybir

K, T, S, V, N, H = 512, 2048, 512, 256, 512, 512
FLOPS = 2 * S * (K * H + H * H + H * N)

F32 = mybir.dt.float32
BF16 = mybir.dt.bfloat16
I32 = mybir.dt.int32
U32 = mybir.dt.uint32
U16 = mybir.dt.uint16
U8 = mybir.dt.uint8
FP8X4 = mybir.dt.float8_e4m3fn_x4
ALU = mybir.AluOpType
ACT = mybir.ActivationFunctionType

P = 128
PACK = 4
HALF = S // 2
QUARTER = S // 4
LIST_ROWS = 16
SLOT = (0, 2, 1, 3)
W1_ON_SCALAR = 80
CAST_PIECES = 4


def tile_picked_lifted_none_p_kernel(
    tc, x_words, x_scales, w1, w2, w3, res, offs, la, lb, ma, mb, out
):
    nc = tc.nc
    with ExitStack() as ctx:
        lists = ctx.enter_context(tc.tile_pool(name="lists", bufs=1))
        sb = ctx.enter_context(tc.tile_pool(name="sb", bufs=1))
        psum = ctx.enter_context(tc.psum_pool(name="psum", bufs=1))

        def alloc(shape, dtype, name, takes_over=None):
            return sb.tile(shape, dtype, name=name, tag=takes_over or name, align_bytes=64)

        def bank(b, name):
            return psum.tile([P, S], F32, name=name, tag="bank%d" % b)

        def load_list(src, name):
            offsets = lists.tile(list(src.shape), U16, name=name)
            nc.sync.dma_start(offsets[:], src)
            return offsets

        def load_weight(w, name):
            raw = alloc([P, PACK, w.shape[1]], F32, name)
            nc.sync.dma_start(raw[:], w.rearrange("(p j) c -> p j c", j=PACK))
            return raw

        def dealt_views(rounded, raw):
            return (
                rounded[:].rearrange("p (a b m j) -> p m b a j", a=2, b=2, j=PACK),
                raw[:].rearrange("p j (m b a) -> p m b a j", a=2, b=2),
            )

        def quantise_weight(rounded, first, count, name, takes_over=None, scales=None):
            codes = alloc([P, count * P], U32, name + "_codes", takes_over)
            if scales is None:
                scales = alloc([P, count * P], U8, name + "_scales")[:]
            nc.vector.quantize_mx(
                out=codes[:].bitcast(FP8X4), scales=scales, in_=rounded[:, first * PACK * P : (first + count) * PACK * P]
            )
            return [(codes[:, g * P : (g + 1) * P], scales[:, g * P : (g + 1) * P]) for g in range(count)]

        def quantise_places(halves, codes, scales, first, count):
            cols = slice(first * QUARTER, (first + count) * QUARTER)
            words = halves[first // 2][:].rearrange("p n j -> p (n j)")
            nc.vector.quantize_mx(
                out=codes[:, cols].bitcast(FP8X4),
                scales=scales[:, cols],
                in_=words[:, (first % 2) * PACK * QUARTER : (first % 2 + count) * PACK * QUARTER],
            )

        def product(dst, weight, codes, scales):
            nc.tensor.matmul_mx(
                out=dst, lhsT=weight[0].bitcast(FP8X4), lhsT_scale=weight[1],
                rhs=codes.bitcast(FP8X4), rhs_scale=scales, start=True, stop=True,
            )

        def product_to_rows(b, name, rows, cols, weight, codes, scales):
            width = cols.stop - cols.start
            acc = bank(b, name)
            product(acc[:, 0:width], weight, codes[:, cols], scales[:, cols])
            nc.scalar.copy(rows[:, cols], acc[:, 0:width])

        def gather(rows, offsets, name, takes_over=None):
            picked = alloc([P, V], F32, name, takes_over)
            nc.vector.tensor_copy(picked[:], rows[:].indirect(offsets[:]))
            return picked

        def gather_less(rows, offsets, other, name, takes_over=None):
            diff = alloc([P, V], F32, name, takes_over)
            nc.vector.tensor_tensor(diff[:], rows[:].indirect(offsets[:]), other[:], ALU.subtract)
            return diff

        def apply(func, scale, src, name, takes_over=None):
            dst = alloc([P, V], F32, name, takes_over)
            nc.scalar.activation(dst[:], src[:], func, scale=scale)
            return dst

        def scatter_sum(rows, offsets, left, right):
            nc.vector.tensor_tensor(rows[:].indirect(offsets[:]), left[:], right[:], ALU.add)

        def interleave(halves, rows, i):
            for u in range(2):
                nc.scalar.copy(halves[u][:, :, SLOT[i]], rows[:, u * HALF : (u + 1) * HALF])

        def interleave_last(halves, rows):
            for c in range(4):
                dst = halves[c // 2][:, (c % 2) * QUARTER : (c % 2 + 1) * QUARTER, SLOT[3]]
                copy = nc.vector.tensor_copy if c < 2 else nc.scalar.copy
                copy(dst, rows[:, c * QUARTER : (c + 1) * QUARTER])

        x_scale_rows = alloc([P, T], U8, "x_scale_rows")
        nc.vector.memset(x_scale_rows[:].bitcast(I32), 0)
        w1_raw = load_weight(w1, "w1_raw")
        offs_t = load_list(offs, "offs_t")
        for r in range(4):
            nc.sync.dma_start(x_scale_rows[r:P:32, :].bitcast(I32), x_scales[0, r:16:4, :].bitcast(I32))
        x_table = alloc([P, T], I32, "x_table")
        nc.sync.dma_start(x_table[:], x_words[0].rearrange("p n t -> p (n t)").bitcast(I32))
        la_t = load_list(la, "la_t")
        lb_t = load_list(lb, "lb_t")
        w2_raw = load_weight(w2, "w2_raw")
        ma_t = load_list(ma, "ma_t")
        mb_t = load_list(mb, "mb_t")
        w3_raw = load_weight(w3, "w3_raw")
        res_t = alloc([P, N // P, S], F32, "res_t")
        nc.sync.dma_start(res_t[:], res.rearrange("(t p) c -> p t c", p=P))

        w1_bf = alloc([P, PACK * H], BF16, "w1_bf")
        w1_dst, w1_src = dealt_views(w1_bf, w1_raw)
        nc.scalar.copy(w1_dst[:, 0:W1_ON_SCALAR], w1_src[:, 0:W1_ON_SCALAR])
        nc.vector.tensor_copy(w1_dst[:, W1_ON_SCALAR:P], w1_src[:, W1_ON_SCALAR:P])
        x_scales_picked = alloc([P, S], U8, "x_scales_picked")
        nc.vector.tensor_copy(x_scales_picked[:], x_scale_rows[:].indirect(offs_t[:]))
        w1_q = quantise_weight(w1_bf, 0, 2, "w1_01") + quantise_weight(w1_bf, 2, 1, "w1_2") + quantise_weight(w1_bf, 3, 1, "w1_3")
        x_picked = alloc([P, S], U32, "x_picked")
        y = [alloc([P, S], F32, "y%d" % i) for i in range(PACK)]
        for u in range(2):
            cols = slice(u * HALF, (u + 1) * HALF)
            entries = slice(u * HALF // LIST_ROWS, (u + 1) * HALF // LIST_ROWS)
            nc.vector.tensor_copy(x_picked[:, cols], x_table[:].bitcast(U32).indirect(offs_t[:, entries]))
            for i in range(2):
                product_to_rows(2 * u + i, "y_acc%d%d" % (i, u), y[i], cols, w1_q[i], x_picked, x_scales_picked)
        for i in range(2, PACK):
            product_to_rows(2 + i, "y_acc%d" % i, y[i], slice(0, S), w1_q[i], x_picked, x_scales_picked)

        z = [alloc([P, S], F32, "z%d" % i) for i in range(PACK)]
        z_bf = [alloc([P, HALF, PACK], BF16, "z_bf%d" % u) for u in range(2)]
        handed_on = ("w1_2_codes", "w1_2_scales")
        ya, yd, yd_half = {}, {}, {}

        def lift_second_gathers(tiles, buffers):
            for i, buffer in zip(tiles, buffers):
                yd[i] = gather_less(y[i], lb_t, ya[i], "yd%d" % i, buffer)
                yd_half[i] = apply(ACT.Copy, 0.5, yd[i], "yd_half%d" % i, "yd_half%d" % (i % 2))

        def lift_first_scatters(tiles):
            for i in tiles:
                nc.vector.tensor_copy(z[i][:].indirect(la_t[:]), yd[i][:])

        for i in (0, 1):
            ya[i] = gather(y[i], la_t, "ya%d" % i)
        lift_second_gathers((0, 1), handed_on)
        w2_bf = alloc([P, PACK * H], BF16, "w2_bf", "w1_01_codes")
        w3_bf = alloc([P, PACK * N], BF16, "w3_bf")
        w2_views = dealt_views(w2_bf, w2_raw)
        w3_views = (
            w3_bf[:].rearrange("p (c i j) -> p c j i", i=4, j=PACK),
            w3_raw[:].rearrange("p j (c i) -> p c j i", i=4),
        )
        for dst, src in (w2_views, w3_views):
            for piece in range(CAST_PIECES):
                groups = slice(piece * P // CAST_PIECES, (piece + 1) * P // CAST_PIECES)
                nc.scalar.copy(dst[:, groups], src[:, groups])
        lift_first_scatters((0, 1))
        for i in (0, 1):
            scatter_sum(z[i], lb_t, ya[i], yd_half[i])
            interleave(z_bf, z[i], i)
        for i in (2, 3):
            ya[i] = gather(y[i], la_t, "ya%d" % i, handed_on[i - 2])
        lift_second_gathers((2, 3), ("ya0", "ya1"))
        lift_first_scatters((2, 3))
        scatter_sum(z[2], lb_t, ya[2], yd_half[2])
        interleave(z_bf, z[2], 2)
        scatter_sum(z[3], lb_t, ya[3], yd_half[3])
        w2_q = quantise_weight(w2_bf, 0, 2, "w2_01", handed_on[0])
        interleave_last(z_bf, z[3])

        z_codes = alloc([P, S], U32, "z_codes")
        z_scales = alloc([P, S], U8, "z_scales")
        h = [alloc([P, S], F32, "h%d" % i) for i in range(PACK)]
        for b, (first, count) in enumerate(((0, 2), (2, 1), (3, 1))):
            acc = bank(b, "h_acc0%d" % first)
            for c in range(first, first + count):
                cols = slice(c * QUARTER, (c + 1) * QUARTER)
                quantise_places(z_bf, z_codes, z_scales, c, 1)
                product(acc[:, (c - first) * QUARTER : (c - first + 1) * QUARTER], w2_q[0], z_codes[:, cols], z_scales[:, cols])
            nc.scalar.copy(h[0][:, first * QUARTER : (first + count) * QUARTER], acc[:, 0 : count * QUARTER])
        late_scales = alloc([P, 4 * P], U8, "late_scales", "z_bf1")
        for i in range(2, PACK):
            w2_q += quantise_weight(w2_bf, i, 1, "w2_%d" % i, scales=late_scales[:, (i - 2) * P : (i - 1) * P])
        for u in range(2):
            product_to_rows(3 + u, "h_acc1%d" % u, h[1], slice(u * HALF, (u + 1) * HALF), w2_q[1], z_codes, z_scales)
        for i in range(2, PACK):
            product_to_rows(3 + i, "h_acc%d" % i, h[i], slice(0, S), w2_q[i], z_codes, z_scales)
        w3_q = quantise_weight(w3_bf, 0, 2, "w3_01", scales=late_scales[:, 2 * P : 4 * P])

        z2 = [alloc([P, S], F32, "z2%d" % i) for i in range(PACK)]
        z2_bf = [alloc([P, HALF, PACK], BF16, "z2_bf%d" % u) for u in range(2)]
        ha, hd, rise, fall = {}, {}, {}, {}

        def sort_second_gathers(tiles, buffers):
            for i, buffer in zip(tiles, buffers):
                hd[i] = gather_less(h[i], mb_t, ha[i], "hd%d" % i, buffer)
                rise[i] = apply(ACT.Relu, 1.0, hd[i], "rise%d" % i, "rise%d" % (i % 2))

        def sort_first_scatters(tiles):
            drop = {i: apply(ACT.Relu, -1.0, hd[i], "drop%d" % i) for i in tiles}
            for i in tiles:
                fall[i] = apply(ACT.Copy, -1.0, drop[i], "fall%d" % i, "fall%d" % (i % 2))
            for i in tiles:
                scatter_sum(z2[i], ma_t, ha[i], rise[i])

        for i in (0, 1):
            ha[i] = gather(h[i], ma_t, "ha%d" % i)
        sort_second_gathers((0, 1), ("w2_2_codes", None))
        sort_first_scatters((0, 1))
        for i in (2, 3):
            ha[i] = gather(h[i], ma_t, "ha%d" % i, "drop%d" % (i - 2))
        scatter_sum(z2[0], mb_t, ha[0], fall[0])
        interleave(z2_bf, z2[0], 0)
        sort_second_gathers((2, 3), (None, None))
        scatter_sum(z2[1], mb_t, ha[1], fall[1])
        interleave(z2_bf, z2[1], 1)
        sort_first_scatters((2, 3))
        scatter_sum(z2[2], mb_t, ha[2], fall[2])
        interleave(z2_bf, z2[2], 2)
        scatter_sum(z2[3], mb_t, ha[3], fall[3])
        w3_q += quantise_weight(w3_bf, 2, 2, "w3_23", "drop0")
        interleave_last(z2_bf, z2[3])

        z2_codes = alloc([P, S], U32, "z2_codes")
        z2_scales = alloc([P, S], U8, "z2_scales")
        for first, count in ((0, 1), (1, 1), (2, 2)):
            quantise_places(z2_bf, z2_codes, z2_scales, first, count)
        for u in range(2):
            cols = slice(u * HALF, (u + 1) * HALF)
            for t in range(N // P):
                acc = bank(4 * u + t, "out_acc%d%d" % (u, t))
                product(acc[:, 0:HALF], w3_q[t], z2_codes[:, cols], z2_scales[:, cols])
                summed = alloc([P, HALF], F32, "summed%d%d" % (u, t))
                nc.vector.tensor_tensor(summed[:], acc[:, 0:HALF], res_t[:, t, cols], ALU.add)
                nc.sync.dma_start(out[t * P : (t + 1) * P, cols], summed[:])
